import numpy as np
import ml_dtypes


def mxq(x, axis, fmt="e4m3"):
    dtype, down = {"e4m3": (ml_dtypes.float8_e4m3fn, 7), "e5m2": (ml_dtypes.float8_e5m2, 14)}[fmt]
    v = np.moveaxis(np.asarray(x, np.float32).astype(ml_dtypes.bfloat16).astype(np.float64), axis, -1)
    blocks = v.reshape(v.shape[:-1] + (-1, 32))
    amax = np.abs(blocks).max(-1, keepdims=True)
    byte = np.maximum(np.where(amax > 0, np.frexp(amax)[1] - 1 + 127, 0) - down, 1)
    scale = np.exp2(byte - 127.0)
    codes = (blocks / scale).astype(np.float32).astype(dtype).astype(np.float64)
    return np.moveaxis((codes * scale).reshape(v.shape), -1, axis)


WIDE = False


def mx_kscale(k):
    if not WIDE:
        return np.ones(k)
    levels = np.array([10, -10, 5, -5, 0])
    if k % 512:
        return np.exp2(np.random.permutation(np.resize(levels, k // 32))).repeat(32)
    a = np.empty((k // 512, 16))
    for p in range(k // 512):
        a[p, :8] = np.random.permutation(np.resize(levels, 8))
        for g in range(8):
            far = levels[np.abs(levels - a[p, g]) >= 10]
            a[p, g + 8] = far[np.random.randint(len(far))]
    return np.exp2(a.ravel()).repeat(32)


def f64(x):
    return np.asarray(x).astype(np.float64)


def striped(idx):
    return np.tile(np.asarray(idx).reshape(-1, 16).T, (8, 1)).astype(np.uint16)


def unstriped(offs):
    return offs[:16].T.reshape(-1).astype(np.int64)


E2M1 = np.array([0.0, 0.5, 1.0, 1.5, 2.0, 3.0, 4.0, 6.0, -0.0, -0.5, -1.0, -1.5, -2.0, -3.0, -4.0, -6.0])


def pack_weight(w, fmt):
    k, n = w.shape
    w = f64(np.asarray(w, np.float32).astype(ml_dtypes.bfloat16)).reshape(k // 32, 32, n)
    amax = np.abs(w).max(1)
    if fmt == "e4m3":
        byte = np.frexp(amax)[1] - 1 + 127 - 7
    else:
        mant, ex = np.frexp(amax / 6.0)
        byte = np.where(mant > 0.5, ex, ex - 1) + 127
    byte = np.clip(np.where(amax > 0, byte, 1), 1, 254)
    scaled = (w * np.exp2(127.0 - byte)[:, None, :]).reshape(k, n).astype(np.float32)
    by_word = np.ascontiguousarray(scaled.reshape(k // 512, 128, 4, n).transpose(0, 1, 3, 2))
    if fmt == "e4m3":
        words = by_word.astype(ml_dtypes.float8_e4m3fn).view(np.uint8)
    else:
        c = by_word.astype(ml_dtypes.float4_e2m1fn).view(np.uint8) & 0xF
        words = (c[..., 0::2] | (c[..., 1::2] << 4)).reshape(k // 512, 128, 2 * n)
    return np.ascontiguousarray(words), np.ascontiguousarray(byte.astype(np.uint8).reshape(k // 512, 16, n))


def unpack_weight(words, scales, fmt):
    g, _, n = scales.shape
    words = np.ascontiguousarray(words).reshape(g, 128, n, -1)
    if fmt == "e4m3":
        vals = words.view(ml_dtypes.float8_e4m3fn).astype(np.float64)
    else:
        nib = np.empty((g, 128, n, 4), np.uint8)
        nib[..., 0::2] = words & 0xF
        nib[..., 1::2] = words >> 4
        vals = E2M1[nib]
    vals = vals * np.repeat(np.exp2(scales.astype(np.float64) - 127.0), 8, axis=1)[..., None]
    return vals.transpose(0, 1, 3, 2).reshape(g * 512, n)


D, T, I, Q, E, K = 512, 2048, 512, 512, 512, 64


def setup_inputs():
    n = np.random.standard_normal
    idx = np.random.permutation(T)[:I]
    fd = mx_kscale(D)
    fi = mx_kscale(I)
    ti = np.ones(T)
    ti[idx] = fi
    keysp = pack_weight(n((D, T)) / fd[:, None], "e4m3")
    return {
        "query": (n((D, Q)) * 0.7 / np.sqrt(D) * fd[:, None]).astype(np.float32),
        "query2": (n((D, Q)) * 0.7 / np.sqrt(D) * fd[:, None]).astype(np.float32),
        "keys_words": keysp[0],
        "keys_scales": keysp[1],
        "xmark": np.tile(np.random.uniform(-1.0, 1.0, T), (128, 1)).astype(np.float32),
        "ymark": np.tile(np.random.uniform(-1.0, 1.0, T), (128, 1)).astype(np.float32),
        "lam": (np.random.uniform(0.5, 1.2, (Q, 1))).astype(np.float32),
        "earlier": (np.random.uniform(0.1, 2.0, (Q, I))).astype(np.float32),
        "trust": (np.random.uniform(0.3, 0.8, (Q, 1))).astype(np.float32),
        "os": (np.random.uniform(4.0, 16.0, (1, I)) * fi).astype(np.float32),
        "vals": (n((E, T)) / ti).astype(np.float32),
        "offs": striped(idx),
    }


def reference(query, query2, keys_words, keys_scales, xmark, ymark, lam, earlier, trust, os, vals, offs):
    idx = unstriped(offs)
    keysu = unpack_weight(keys_words, keys_scales, "e4m3")
    queryq = mxq(f64(query), 0, "e4m3")
    keysidxg = keysu[:, idx]
    a = queryq.T @ keysidxg
    query2q = mxq(f64(query2), 0, "e4m3")
    b = query2q.T @ keysidxg
    dx = a - f64(xmark)[:1][:, idx]
    dy = b - f64(ymark)[:1][:, idx]
    s = (np.square(dx) + np.square(dy)) * f64(lam) * (-1.0)
    p = np.exp(s - np.max(s, axis=1, keepdims=True))
    r = p / np.sum(p, axis=1, keepdims=True)
    re0 = f64(earlier) / np.sum(f64(earlier), axis=1, keepdims=True)
    w = r * f64(trust) + re0 * (1.0 - f64(trust))
    wo1 = w * f64(os)
    wt1 = wo1.T
    wgr = wt1.reshape(I, K, Q // K).sum(axis=2)
    vt1 = f64(vals)[:, idx].T
    vt1q = mxq(vt1, 0, "e4m3")
    wgrq = mxq(wgr, 0, "e4m3")
    o = vt1q.T @ wgrq
    return o

@@ -1,0 +1,308 @@
+from contextlib import ExitStack
+
+import concourse.mybir as mybir
+from concourse.masks import make_identity
+
+D, T, I, Q, E, K = 512, 2048, 512, 512, 512, 64
+FLOPS = 2 * (2 * D * Q * I + I * E * K)
+
+F32 = mybir.dt.float32
+BF16 = mybir.dt.bfloat16
+I32 = mybir.dt.int32
+U32 = mybir.dt.uint32
+U16 = mybir.dt.uint16
+U8 = mybir.dt.uint8
+FP8X4 = mybir.dt.float8_e4m3fn_x4
+ALU = mybir.AluOpType
+ACT = mybir.ActivationFunctionType
+AX = mybir.AxisListType
+
+P = 128
+PACK = 4
+
+
+def tile_attend_maplace_carried_sharedrows_kernel(
+    tc, query, query2, keys_words, keys_scales, xmark, ymark, lam, earlier, trust, slot_factor, vals, offs, out
+):
+    nc = tc.nc
+    with ExitStack() as ctx:
+        keep = ctx.enter_context(tc.tile_pool(name="keep", bufs=1))
+        psum = ctx.enter_context(tc.psum_pool(name="psum", bufs=1))
+
+        def sb(name, shape, dtype, tag=None):
+            return keep.tile(shape, dtype, name=name, tag=tag or name, align_bytes=64)
+
+        def bank(name, shape, tag):
+            return psum.tile(shape, F32, name=name, tag=tag)
+
+        offsets = keep.tile([P, I // 16], U16, name="offsets")
+        nc.sync.dma_start(offsets[:], offs)
+
+        ident = sb("ident", [P, P], F32)
+        make_identity(nc, ident[:])
+        mark_pools = []
+
+        def load_mark(name, mark, engine):
+            pool_tile = sb(name, [P, T], F32)
+            engine.memset(pool_tile[: P - 1, :], 0.0)
+            nc.sync.dma_start(out=pool_tile[P - 1 :, :], in_=mark[0:1, :])
+            mark_pools.append(pool_tile)
+
+        load_mark("x_pool", xmark, nc.vector)
+        key_scale_pool = sb("key_scale_pool", [P, T], U8)
+        for quad in range(4):
+            rows = keys_scales[0, 4 * quad : 4 * quad + 4, :].bitcast(I32)
+            nc.sync.dma_start(
+                out=key_scale_pool[32 * quad : 32 * quad + 32, :].bitcast(I32),
+                in_=rows.unsqueeze(0).to_broadcast([8, 4, T // 4]),
+            )
+        raw_queries = []
+
+        def load_query(name, src):
+            raw = sb(name, [P, PACK, Q], F32)
+            nc.sync.dma_start(out=raw[:], in_=src.rearrange("(p t) q -> p t q", t=PACK))
+            raw_queries.append(raw)
+
+        load_query("q_raw", query)
+        load_mark("y_pool", ymark, nc.gpsimd)
+        key_word_pool = sb("key_word_pool", [P, T], U32)
+        nc.sync.dma_start(
+            out=key_word_pool[:].bitcast(I32), in_=keys_words[0].rearrange("p n t -> p (n t)").bitcast(I32)
+        )
+        lam_sb = sb("lam_sb", [P, 4], F32)
+        nc.sync.dma_start(out=lam_sb[:], in_=lam.rearrange("(m j) o -> m (j o)", j=4))
+        trust_sb = sb("trust_sb", [P, 4], F32)
+        nc.sync.dma_start(out=trust_sb[:], in_=trust.rearrange("(m j) o -> m (j o)", j=4))
+        factor_sb = sb("factor_sb", [P, PACK], F32)
+        nc.sync.dma_start(out=factor_sb[:], in_=slot_factor.rearrange("o (p t) -> p (o t)", t=PACK))
+
+        load_query("q2_raw", query2)
+
+        mark_cols = []
+        for name, pool_tile, tag in (("x", mark_pools[0], "dist0"), ("y", mark_pools[1], "dist3")):
+            listed = sb(name + "_listed", [P, I], F32, tag=name + "_listed")
+            nc.scalar.activation(out=listed[:], in_=pool_tile[:].indirect(offsets[:]), func=ACT.Copy)
+            turned = bank(name + "_turned", [P, 4, P], tag)
+            for c in range(4):
+                nc.tensor.transpose(turned[:, c, :], listed[:, c * P : (c + 1) * P], ident[:])
+            cols = sb(name + "_cols", [P, 4], F32)
+            nc.scalar.copy(out=cols[:], in_=turned[:, :, P - 1])
+            mark_cols.append(cols)
+
+        earlier_sb = sb("earlier_sb", [P, 4, I], F32)
+        nc.sync.dma_start(out=earlier_sb[:], in_=earlier.rearrange("(m j) i -> m j i", j=4))
+        val_pools = []
+        vals_by_row = vals.rearrange("(r j) t -> r j t", j=4)
+
+        def load_vals(j):
+            val_pools.append(sb("val_pool%d" % j, [P, T], F32))
+            nc.sync.dma_start(out=val_pools[j][:], in_=vals_by_row[:, j, :])
+
+        load_vals(0)
+        load_vals(1)
+
+        distrust = sb("distrust", [P, 4], F32)
+        nc.vector.tensor_scalar(
+            out=distrust[:], in0=trust_sb[:], scalar1=-1.0, scalar2=1.0, op0=ALU.mult, op1=ALU.add
+        )
+
+        dist = [None] * 4
+
+        def quantise_query(n):
+            woven = sb("q_woven%d" % n, [P, Q, PACK], BF16, tag="woven%d" % n)
+            nc.vector.tensor_copy(
+                out=woven[:].rearrange("p (c i) t -> p c t i", i=4),
+                in_=raw_queries[n][:].rearrange("p t (c i) -> p c t i", i=4),
+            )
+            load_vals(2 + n)
+            words = sb("q_words%d" % n, [P, Q], U32)
+            scales = sb("q_scales%d" % n, [P, Q], U8)
+            nc.vector.quantize_mx(
+                out=words[:].bitcast(FP8X4), scales=scales[:], in_=woven[:].rearrange("p q t -> p (q t)")
+            )
+            return words, scales
+
+        def scores(n, c, words, scales):
+            acc = bank("score%d_%d" % (n, c), [P, Q], "score%d" % c)
+            cols = slice(c * P, (c + 1) * P)
+            nc.tensor.matmul_mx(
+                out=acc[:],
+                lhsT=key_words[:, cols].bitcast(FP8X4),
+                lhsT_scale=key_scales[:, cols],
+                rhs=words[:].bitcast(FP8X4),
+                rhs_scale=scales[:],
+                start=True,
+                stop=True,
+            )
+            return acc
+
+        def square(n, c, acc, sq, js):
+            nc.scalar.activation(
+                out=sq[:, js, :],
+                in_=acc[:].rearrange("p (m j) -> p j m", j=4)[:, js, :],
+                func=ACT.Square,
+                scale=-1.0,
+                bias=mark_cols[n][:, c : c + 1],
+            )
+
+        def turn_square(n, c, sq, j):
+            nc.tensor.matmul(
+                out=dist[j][:, c * P : (c + 1) * P],
+                lhsT=sq[:, j, :],
+                rhs=ident[:],
+                is_transpose=True,
+                start=(n == 0 and c == 0),
+                stop=(n == 1 and c == 3),
+            )
+
+        words, scales = quantise_query(0)
+        key_scales = sb("key_scales", [P, I], U8)
+        nc.vector.tensor_copy(out=key_scales[:], in_=key_scale_pool[:].indirect(offsets[:]))
+        key_words = sb("key_words", [P, I], U32)
+        for half in range(2):
+            nc.vector.tensor_copy(
+                out=key_words[:, half * I // 2 : (half + 1) * I // 2],
+                in_=key_word_pool[:].indirect(offsets[:, half * I // 32 : (half + 1) * I // 32]),
+            )
+
+        accs = [scores(0, c, words, scales) for c in range(4)]
+        for j in range(4):
+            dist[j] = bank("dist_%d" % j, [P, I], "dist%d" % j)
+        words2, scales2 = quantise_query(1)
+        sqs = [sb("sqx%d" % c, [P, 4, P], F32) for c in range(4)]
+        for c in range(4):
+            square(0, c, accs[c], sqs[c], slice(0, 4))
+        accs = [scores(1, c, words2, scales2) for c in range(4)]
+        for c in range(4):
+            for j in range(4):
+                turn_square(0, c, sqs[c], j)
+        sqs = [sb("sqy%d" % c, [P, 4, P], F32) for c in range(4)]
+        for half in range(2):
+            for c in range(4):
+                square(1, c, accs[c], sqs[c], slice(2 * half, 2 * half + 2))
+                for j in (2 * half, 2 * half + 1):
+                    turn_square(1, c, sqs[c], j)
+
+        earlier_sum = sb("earlier_sum", [P, 4], F32)
+        for j in range(4):
+            nc.vector.tensor_reduce(out=earlier_sum[:, j : j + 1], in_=earlier_sb[:, j, :], axis=AX.X, op=ALU.add)
+
+        scaled = []
+        least = []
+        probs = []
+        sums = []
+        for j in range(4):
+            scaled.append(sb("scaled%d" % j, [P, PACK, P], F32))
+            least.append(sb("least%d" % j, [P, 1], F32))
+            nc.vector.tensor_scalar(
+                out=scaled[j][:],
+                in0=dist[j][:].rearrange("p (m t) -> p t m", t=PACK),
+                scalar1=lam_sb[:, j : j + 1],
+                scalar2=None,
+                op0=ALU.mult,
+                op1=ALU.min,
+                accum_out=least[j][:],
+            )
+            probs.append(sb("prob%d" % j, [P, PACK, P], F32))
+            sums.append(sb("sum%d" % j, [P, 1], F32))
+            nc.scalar.activation(
+                out=probs[j][:], in_=scaled[j][:], func=ACT.Exp, scale=-1.0, bias=least[j][:], accum_out=sums[j][:]
+            )
+
+        earlier_inv = sb("earlier_inv", [P, 4], F32)
+        nc.vector.reciprocal(out=earlier_inv[:], in_=earlier_sum[:])
+        carried = []
+        for j in range(4):
+            carried.append(sb("carried%d" % j, [P, PACK, P], F32))
+            nc.vector.tensor_scalar(
+                out=carried[j][:].rearrange("p t m -> p m t"),
+                in0=earlier_sb[:, j, :].rearrange("p (m t) -> p m t", t=PACK),
+                scalar1=earlier_inv[:, j : j + 1],
+                scalar2=distrust[:, j : j + 1],
+                op0=ALU.mult,
+                op1=ALU.mult,
+            )
+
+        weights = bank("weights", [P, PACK, P], "score0")
+
+        def add_turned(src, first, last):
+            for t in range(PACK):
+                nc.tensor.matmul(
+                    out=weights[:, t, :],
+                    lhsT=src[:, t, :],
+                    rhs=ident[:],
+                    is_transpose=True,
+                    start=(first and t == 0),
+                    stop=(last and t == PACK - 1),
+                )
+
+        for j in range(4):
+            add_turned(carried[j], j == 0, False)
+
+        for j in range(4):
+            inv = sb("inv%d" % j, [P, 1], F32)
+            nc.vector.reciprocal(out=inv[:], in_=sums[j][:])
+            share = sb("share%d" % j, [P, PACK, P], F32)
+            nc.vector.tensor_scalar(
+                out=share[:],
+                in0=probs[j][:],
+                scalar1=inv[:],
+                scalar2=trust_sb[:, j : j + 1],
+                op0=ALU.mult,
+                op1=ALU.mult,
+            )
+            add_turned(share, False, j == 3)
+
+        grouped = sb("grouped", [P, K, PACK], F32)
+        nc.vector.tensor_reduce(
+            out=grouped[:], in_=weights[:].rearrange("p t (k h) -> p k t h", h=2), axis=AX.X, op=ALU.add
+        )
+        grouped_bf = sb("grouped_bf", [P, K, PACK], BF16)
+        nc.vector.tensor_tensor(
+            out=grouped_bf[:], in0=grouped[:], in1=factor_sb[:].unsqueeze(1).to_broadcast([P, K, PACK]), op=ALU.mult
+        )
+        w_words = sb("w_words", [P, K], U32)
+        w_scales = sb("w_scales", [P, K], U8)
+        nc.vector.quantize_mx(
+            out=w_words[:].bitcast(FP8X4), scales=w_scales[:], in_=grouped_bf[:].rearrange("p k t -> p (k t)")
+        )
+
+        val_operands = []
+        half_cols = I // 32
+        for j in range(4):
+            listed = sb("val_listed%d" % j, [P, I], BF16, tag=("scaled3", "least3", None, None)[j])
+            window = val_pools[j][:]
+            if j < 3:
+                nc.scalar.activation(out=listed[:], in_=window.indirect(offsets[:]), func=ACT.Copy)
+            else:
+                nc.scalar.activation(
+                    out=listed[:, : I // 2], in_=window.indirect(offsets[:, :half_cols]), func=ACT.Copy
+                )
+                nc.vector.tensor_copy(out=listed[:, I // 2 :], in_=window.indirect(offsets[:, half_cols:]))
+            pairs = listed[:].bitcast(F32)
+            turned = bank("val_turned%d" % j, [P, 2, P], "score%d" % (1 + j % 3))
+            for u in range(2):
+                nc.tensor.transpose(turned[:, u, :], pairs[:, u::2], ident[:])
+            woven = sb("val_woven%d" % j, [P, P * PACK], BF16)
+            nc.vector.tensor_copy(
+                out=woven[:].bitcast(F32).rearrange("p (r u) -> p r u", u=2), in_=turned[:].rearrange("p u r -> p r u")
+            )
+            words = sb("val_words%d" % j, [P, P], U32)
+            scales = sb("val_scales%d" % j, [P, P], U8)
+            nc.vector.quantize_mx(out=words[:].bitcast(FP8X4), scales=scales[:], in_=woven[:])
+            val_operands.append((words, scales))
+
+        result = bank("result", [P, 4, K], "dist0")
+        for j, (words, scales) in enumerate(val_operands):
+            nc.tensor.matmul_mx(
+                out=result[:, j, :],
+                lhsT=words[:].bitcast(FP8X4),
+                lhsT_scale=scales[:],
+                rhs=w_words[:].bitcast(FP8X4),
+                rhs_scale=w_scales[:],
+                start=True,
+                stop=True,
+            )
+        result_sb = sb("result_sb", [P, 4, K], F32)
+        nc.scalar.copy(out=result_sb[:], in_=result[:])
+        nc.sync.dma_start(out=out.rearrange("(r j) k -> r j k", j=4), in_=result_sb[:])

@@ -38,6 +38,8 @@ def tile_attend_maplace_carried_sharedrows_kernel(
         offsets = keep.tile([P, I // 16], U16, name="offsets")
         nc.sync.dma_start(offsets[:], offs)
 
+        key_scale_pool = sb("key_scale_pool", [P, T], U8)
+        nc.gpsimd.memset(key_scale_pool[:].bitcast(I32), 0)
         ident = sb("ident", [P, P], F32)
         make_identity(nc, ident[:])
         mark_pools = []
@@ -49,12 +51,10 @@ def tile_attend_maplace_carried_sharedrows_kernel(
             mark_pools.append(pool_tile)
 
         load_mark("x_pool", xmark, nc.vector)
-        key_scale_pool = sb("key_scale_pool", [P, T], U8)
         for quad in range(4):
-            rows = keys_scales[0, 4 * quad : 4 * quad + 4, :].bitcast(I32)
-            nc.sync.dma_start(
-                out=key_scale_pool[32 * quad : 32 * quad + 32, :].bitcast(I32),
-                in_=rows.unsqueeze(0).to_broadcast([8, 4, T // 4]),
+            nc.scalar.dma_start(
+                out=key_scale_pool[32 * quad : 32 * quad + 4, :].bitcast(I32),
+                in_=keys_scales[0, 4 * quad : 4 * quad + 4, :].bitcast(I32),
             )
         raw_queries = []
 
@@ -65,10 +65,11 @@ def tile_attend_maplace_carried_sharedrows_kernel(
 
         load_query("q_raw", query)
         load_mark("y_pool", ymark, nc.gpsimd)
-        key_word_pool = sb("key_word_pool", [P, T], U32)
+        key_word_pool = sb("key_word_pool", [P, T], U32, tag="woven1")
         nc.sync.dma_start(
             out=key_word_pool[:].bitcast(I32), in_=keys_words[0].rearrange("p n t -> p (n t)").bitcast(I32)
         )
+        load_query("q2_raw", query2)
         lam_sb = sb("lam_sb", [P, 4], F32)
         nc.sync.dma_start(out=lam_sb[:], in_=lam.rearrange("(m j) o -> m (j o)", j=4))
         trust_sb = sb("trust_sb", [P, 4], F32)
@@ -76,7 +77,6 @@ def tile_attend_maplace_carried_sharedrows_kernel(
         factor_sb = sb("factor_sb", [P, PACK], F32)
         nc.sync.dma_start(out=factor_sb[:], in_=slot_factor.rearrange("o (p t) -> p (o t)", t=PACK))
 
-        load_query("q2_raw", query2)
 
         mark_cols = []
         for name, pool_tile, tag in (("x", mark_pools[0], "dist0"), ("y", mark_pools[1], "dist3")):
@@ -98,8 +98,8 @@ def tile_attend_maplace_carried_sharedrows_kernel(
             val_pools.append(sb("val_pool%d" % j, [P, T], F32))
             nc.sync.dma_start(out=val_pools[j][:], in_=vals_by_row[:, j, :])
 
-        load_vals(0)
-        load_vals(1)
+        for j in range(4):
+            load_vals(j)
 
         distrust = sb("distrust", [P, 4], F32)
         nc.vector.tensor_scalar(
@@ -108,13 +108,15 @@ def tile_attend_maplace_carried_sharedrows_kernel(
 
         dist = [None] * 4
 
-        def quantise_query(n):
+        def weave_query(n):
             woven = sb("q_woven%d" % n, [P, Q, PACK], BF16, tag="woven%d" % n)
             nc.vector.tensor_copy(
                 out=woven[:].rearrange("p (c i) t -> p c t i", i=4),
                 in_=raw_queries[n][:].rearrange("p t (c i) -> p c t i", i=4),
             )
-            load_vals(2 + n)
+            return woven
+
+        def quantise_query(n, woven):
             words = sb("q_words%d" % n, [P, Q], U32)
             scales = sb("q_scales%d" % n, [P, Q], U8)
             nc.vector.quantize_mx(
@@ -155,10 +157,11 @@ def tile_attend_maplace_carried_sharedrows_kernel(
                 stop=(n == 1 and c == 3),
             )
 
-        words, scales = quantise_query(0)
-        key_scales = sb("key_scales", [P, I], U8)
+        woven = weave_query(0)
+        key_scales = sb("key_scales", [P, I], U8, tag="q_raw")
         nc.vector.tensor_copy(out=key_scales[:], in_=key_scale_pool[:].indirect(offsets[:]))
-        key_words = sb("key_words", [P, I], U32)
+        words, scales = quantise_query(0, woven)
+        key_words = sb("key_words", [P, I], U32, tag="woven0")
         for half in range(2):
             nc.vector.tensor_copy(
                 out=key_words[:, half * I // 2 : (half + 1) * I // 2],
@@ -168,7 +171,7 @@ def tile_attend_maplace_carried_sharedrows_kernel(
         accs = [scores(0, c, words, scales) for c in range(4)]
         for j in range(4):
             dist[j] = bank("dist_%d" % j, [P, I], "dist%d" % j)
-        words2, scales2 = quantise_query(1)
+        words2, scales2 = quantise_query(1, weave_query(1))
         sqs = [sb("sqx%d" % c, [P, 4, P], F32) for c in range(4)]
         for c in range(4):
             square(0, c, accs[c], sqs[c], slice(0, 4))
@@ -183,7 +186,7 @@ def tile_attend_maplace_carried_sharedrows_kernel(
                 for j in (2 * half, 2 * half + 1):
                     turn_square(1, c, sqs[c], j)
 
-        earlier_sum = sb("earlier_sum", [P, 4], F32)
+        earlier_sum = sb("earlier_sum", [P, 4], F32, tag="woven1")
         for j in range(4):
             nc.vector.tensor_reduce(out=earlier_sum[:, j : j + 1], in_=earlier_sb[:, j, :], axis=AX.X, op=ALU.add)
 
@@ -267,13 +270,17 @@ def tile_attend_maplace_carried_sharedrows_kernel(
             out=w_words[:].bitcast(FP8X4), scales=w_scales[:], in_=grouped_bf[:].rearrange("p k t -> p (k t)")
         )
 
-        val_operands = []
         half_cols = I // 32
+        listed_tags = ("scaled3", "least3", "prob3", "val_pool2")
+        woven_early = sb("val_woven_early", [P, 3, P * PACK], BF16)
+        woven_last = sb("val_woven_last", [P, 1, P * PACK], BF16)
         for j in range(4):
-            listed = sb("val_listed%d" % j, [P, I], BF16, tag=("scaled3", "least3", None, None)[j])
+            listed = sb("val_listed%d" % j, [P, I], BF16, tag=listed_tags[j])
             window = val_pools[j][:]
-            if j < 3:
+            if j < 2:
                 nc.scalar.activation(out=listed[:], in_=window.indirect(offsets[:]), func=ACT.Copy)
+            elif j == 2:
+                nc.vector.tensor_copy(out=listed[:], in_=window.indirect(offsets[:]))
             else:
                 nc.scalar.activation(
                     out=listed[:, : I // 2], in_=window.indirect(offsets[:, :half_cols]), func=ACT.Copy
@@ -283,21 +290,26 @@ def tile_attend_maplace_carried_sharedrows_kernel(
             turned = bank("val_turned%d" % j, [P, 2, P], "score%d" % (1 + j % 3))
             for u in range(2):
                 nc.tensor.transpose(turned[:, u, :], pairs[:, u::2], ident[:])
-            woven = sb("val_woven%d" % j, [P, P * PACK], BF16)
-            nc.vector.tensor_copy(
-                out=woven[:].bitcast(F32).rearrange("p (r u) -> p r u", u=2), in_=turned[:].rearrange("p u r -> p r u")
+            woven = woven_early[:, j, :] if j < 3 else woven_last[:, 0, :]
+            nc.scalar.copy(
+                out=woven.bitcast(F32).rearrange("p (r u) -> p r u", u=2), in_=turned[:].rearrange("p u r -> p r u")
             )
-            words = sb("val_words%d" % j, [P, P], U32)
-            scales = sb("val_scales%d" % j, [P, P], U8)
-            nc.vector.quantize_mx(out=words[:].bitcast(FP8X4), scales=scales[:], in_=woven[:])
-            val_operands.append((words, scales))
+        val_operands = []
+        for name, woven, tiles, tag in (("early", woven_early, 3, "grouped"), ("last", woven_last, 1, None)):
+            words = sb("val_words_" + name, [P, tiles * P], U32, tag=tag)
+            scales = sb("val_scales_" + name, [P, tiles * P], U8)
+            nc.vector.quantize_mx(
+                out=words[:].bitcast(FP8X4), scales=scales[:], in_=woven[:].rearrange("p j w -> p (j w)")
+            )
+            for j in range(tiles):
+                val_operands.append((words[:, j * P : (j + 1) * P], scales[:, j * P : (j + 1) * P]))
 
         result = bank("result", [P, 4, K], "dist0")
         for j, (words, scales) in enumerate(val_operands):
             nc.tensor.matmul_mx(
                 out=result[:, j, :],
-                lhsT=words[:].bitcast(FP8X4),
-                lhsT_scale=scales[:],
+                lhsT=words.bitcast(FP8X4),
+                lhsT_scale=scales,
                 rhs=w_words[:].bitcast(FP8X4),
                 rhs_scale=w_scales[:],
                 start=True,

from contextlib import ExitStack

import concourse.mybir as mybir
from concourse.masks import make_identity

D, T, I, Q, E, K = 512, 2048, 512, 512, 512, 64
FLOPS = 2 * (2 * D * Q * I + I * E * K)

F32 = mybir.dt.float32
BF16 = mybir.dt.bfloat16
I32 = mybir.dt.int32
U32 = mybir.dt.uint32
U16 = mybir.dt.uint16
U8 = mybir.dt.uint8
FP8X4 = mybir.dt.float8_e4m3fn_x4
ALU = mybir.AluOpType
ACT = mybir.ActivationFunctionType
AX = mybir.AxisListType

P = 128
PACK = 4


def tile_attend_maplace_carried_sharedrows_kernel(
    tc, query, query2, keys_words, keys_scales, xmark, ymark, lam, earlier, trust, slot_factor, vals, offs, out
):
    nc = tc.nc
    with ExitStack() as ctx:
        keep = ctx.enter_context(tc.tile_pool(name="keep", bufs=1))
        psum = ctx.enter_context(tc.psum_pool(name="psum", bufs=1))

        def sb(name, shape, dtype, tag=None):
            return keep.tile(shape, dtype, name=name, tag=tag or name, align_bytes=64)

        def bank(name, shape, tag):
            return psum.tile(shape, F32, name=name, tag=tag)

        offsets = keep.tile([P, I // 16], U16, name="offsets")
        nc.sync.dma_start(offsets[:], offs)

        key_scale_pool = sb("key_scale_pool", [P, T], U8)
        nc.gpsimd.memset(key_scale_pool[:].bitcast(I32), 0)
        ident = sb("ident", [P, P], F32)
        make_identity(nc, ident[:])
        mark_pools = []

        def load_mark(name, mark, engine):
            pool_tile = sb(name, [P, T], F32)
            engine.memset(pool_tile[: P - 1, :], 0.0)
            nc.sync.dma_start(out=pool_tile[P - 1 :, :], in_=mark[0:1, :])
            mark_pools.append(pool_tile)

        load_mark("x_pool", xmark, nc.vector)
        for quad in range(4):
            nc.scalar.dma_start(
                out=key_scale_pool[32 * quad : 32 * quad + 4, :].bitcast(I32),
                in_=keys_scales[0, 4 * quad : 4 * quad + 4, :].bitcast(I32),
            )
        raw_queries = []

        def load_query(name, src):
            raw = sb(name, [P, PACK, Q], F32)
            nc.sync.dma_start(out=raw[:], in_=src.rearrange("(p t) q -> p t q", t=PACK))
            raw_queries.append(raw)

        load_query("q_raw", query)
        load_mark("y_pool", ymark, nc.gpsimd)
        key_word_pool = sb("key_word_pool", [P, T], U32, tag="woven1")
        nc.sync.dma_start(
            out=key_word_pool[:].bitcast(I32), in_=keys_words[0].rearrange("p n t -> p (n t)").bitcast(I32)
        )
        load_query("q2_raw", query2)
        lam_sb = sb("lam_sb", [P, 4], F32)
        nc.sync.dma_start(out=lam_sb[:], in_=lam.rearrange("(m j) o -> m (j o)", j=4))
        trust_sb = sb("trust_sb", [P, 4], F32)
        nc.sync.dma_start(out=trust_sb[:], in_=trust.rearrange("(m j) o -> m (j o)", j=4))
        factor_sb = sb("factor_sb", [P, PACK], F32)
        nc.sync.dma_start(out=factor_sb[:], in_=slot_factor.rearrange("o (p t) -> p (o t)", t=PACK))


        mark_cols = []
        for name, pool_tile, tag in (("x", mark_pools[0], "dist0"), ("y", mark_pools[1], "dist3")):
            listed = sb(name + "_listed", [P, I], F32, tag=name + "_listed")
            nc.scalar.activation(out=listed[:], in_=pool_tile[:].indirect(offsets[:]), func=ACT.Copy)
            turned = bank(name + "_turned", [P, 4, P], tag)
            for c in range(4):
                nc.tensor.transpose(turned[:, c, :], listed[:, c * P : (c + 1) * P], ident[:])
            cols = sb(name + "_cols", [P, 4], F32)
            nc.scalar.copy(out=cols[:], in_=turned[:, :, P - 1])
            mark_cols.append(cols)

        earlier_sb = sb("earlier_sb", [P, 4, I], F32)
        nc.sync.dma_start(out=earlier_sb[:], in_=earlier.rearrange("(m j) i -> m j i", j=4))
        val_pools = []
        vals_by_row = vals.rearrange("(r j) t -> r j t", j=4)

        def load_vals(j):
            val_pools.append(sb("val_pool%d" % j, [P, T], F32))
            nc.sync.dma_start(out=val_pools[j][:], in_=vals_by_row[:, j, :])

        for j in range(4):
            load_vals(j)

        distrust = sb("distrust", [P, 4], F32)
        nc.vector.tensor_scalar(
            out=distrust[:], in0=trust_sb[:], scalar1=-1.0, scalar2=1.0, op0=ALU.mult, op1=ALU.add
        )

        dist = [None] * 4

        def weave_query(n):
            woven = sb("q_woven%d" % n, [P, Q, PACK], BF16, tag="woven%d" % n)
            nc.vector.tensor_copy(
                out=woven[:].rearrange("p (c i) t -> p c t i", i=4),
                in_=raw_queries[n][:].rearrange("p t (c i) -> p c t i", i=4),
            )
            return woven

        def quantise_query(n, woven):
            words = sb("q_words%d" % n, [P, Q], U32)
            scales = sb("q_scales%d" % n, [P, Q], U8)
            nc.vector.quantize_mx(
                out=words[:].bitcast(FP8X4), scales=scales[:], in_=woven[:].rearrange("p q t -> p (q t)")
            )
            return words, scales

        def scores(n, c, words, scales):
            acc = bank("score%d_%d" % (n, c), [P, Q], "score%d" % c)
            cols = slice(c * P, (c + 1) * P)
            nc.tensor.matmul_mx(
                out=acc[:],
                lhsT=key_words[:, cols].bitcast(FP8X4),
                lhsT_scale=key_scales[:, cols],
                rhs=words[:].bitcast(FP8X4),
                rhs_scale=scales[:],
                start=True,
                stop=True,
            )
            return acc

        def square(n, c, acc, sq, js):
            nc.scalar.activation(
                out=sq[:, js, :],
                in_=acc[:].rearrange("p (m j) -> p j m", j=4)[:, js, :],
                func=ACT.Square,
                scale=-1.0,
                bias=mark_cols[n][:, c : c + 1],
            )

        def turn_square(n, c, sq, j):
            nc.tensor.matmul(
                out=dist[j][:, c * P : (c + 1) * P],
                lhsT=sq[:, j, :],
                rhs=ident[:],
                is_transpose=True,
                start=(n == 0 and c == 0),
                stop=(n == 1 and c == 3),
            )

        woven = weave_query(0)
        key_scales = sb("key_scales", [P, I], U8, tag="q_raw")
        nc.vector.tensor_copy(out=key_scales[:], in_=key_scale_pool[:].indirect(offsets[:]))
        words, scales = quantise_query(0, woven)
        key_words = sb("key_words", [P, I], U32, tag="woven0")
        for half in range(2):
            nc.vector.tensor_copy(
                out=key_words[:, half * I // 2 : (half + 1) * I // 2],
                in_=key_word_pool[:].indirect(offsets[:, half * I // 32 : (half + 1) * I // 32]),
            )

        accs = [scores(0, c, words, scales) for c in range(4)]
        for j in range(4):
            dist[j] = bank("dist_%d" % j, [P, I], "dist%d" % j)
        words2, scales2 = quantise_query(1, weave_query(1))
        sqs = [sb("sqx%d" % c, [P, 4, P], F32) for c in range(4)]
        for c in range(4):
            square(0, c, accs[c], sqs[c], slice(0, 4))
        accs = [scores(1, c, words2, scales2) for c in range(4)]
        for c in range(4):
            for j in range(4):
                turn_square(0, c, sqs[c], j)
        sqs = [sb("sqy%d" % c, [P, 4, P], F32) for c in range(4)]
        for half in range(2):
            for c in range(4):
                square(1, c, accs[c], sqs[c], slice(2 * half, 2 * half + 2))
                for j in (2 * half, 2 * half + 1):
                    turn_square(1, c, sqs[c], j)

        earlier_sum = sb("earlier_sum", [P, 4], F32, tag="woven1")
        for j in range(4):
            nc.vector.tensor_reduce(out=earlier_sum[:, j : j + 1], in_=earlier_sb[:, j, :], axis=AX.X, op=ALU.add)

        scaled = []
        least = []
        probs = []
        sums = []
        for j in range(4):
            scaled.append(sb("scaled%d" % j, [P, PACK, P], F32))
            least.append(sb("least%d" % j, [P, 1], F32))
            nc.vector.tensor_scalar(
                out=scaled[j][:],
                in0=dist[j][:].rearrange("p (m t) -> p t m", t=PACK),
                scalar1=lam_sb[:, j : j + 1],
                scalar2=None,
                op0=ALU.mult,
                op1=ALU.min,
                accum_out=least[j][:],
            )
            probs.append(sb("prob%d" % j, [P, PACK, P], F32))
            sums.append(sb("sum%d" % j, [P, 1], F32))
            nc.scalar.activation(
                out=probs[j][:], in_=scaled[j][:], func=ACT.Exp, scale=-1.0, bias=least[j][:], accum_out=sums[j][:]
            )

        earlier_inv = sb("earlier_inv", [P, 4], F32)
        nc.vector.reciprocal(out=earlier_inv[:], in_=earlier_sum[:])
        carried = []
        for j in range(4):
            carried.append(sb("carried%d" % j, [P, PACK, P], F32))
            nc.vector.tensor_scalar(
                out=carried[j][:].rearrange("p t m -> p m t"),
                in0=earlier_sb[:, j, :].rearrange("p (m t) -> p m t", t=PACK),
                scalar1=earlier_inv[:, j : j + 1],
                scalar2=distrust[:, j : j + 1],
                op0=ALU.mult,
                op1=ALU.mult,
            )

        weights = bank("weights", [P, PACK, P], "score0")

        def add_turned(src, first, last):
            for t in range(PACK):
                nc.tensor.matmul(
                    out=weights[:, t, :],
                    lhsT=src[:, t, :],
                    rhs=ident[:],
                    is_transpose=True,
                    start=(first and t == 0),
                    stop=(last and t == PACK - 1),
                )

        for j in range(4):
            add_turned(carried[j], j == 0, False)

        for j in range(4):
            inv = sb("inv%d" % j, [P, 1], F32)
            nc.vector.reciprocal(out=inv[:], in_=sums[j][:])
            share = sb("share%d" % j, [P, PACK, P], F32)
            nc.vector.tensor_scalar(
                out=share[:],
                in0=probs[j][:],
                scalar1=inv[:],
                scalar2=trust_sb[:, j : j + 1],
                op0=ALU.mult,
                op1=ALU.mult,
            )
            add_turned(share, False, j == 3)

        grouped = sb("grouped", [P, K, PACK], F32)
        nc.vector.tensor_reduce(
            out=grouped[:], in_=weights[:].rearrange("p t (k h) -> p k t h", h=2), axis=AX.X, op=ALU.add
        )
        grouped_bf = sb("grouped_bf", [P, K, PACK], BF16)
        nc.vector.tensor_tensor(
            out=grouped_bf[:], in0=grouped[:], in1=factor_sb[:].unsqueeze(1).to_broadcast([P, K, PACK]), op=ALU.mult
        )
        w_words = sb("w_words", [P, K], U32)
        w_scales = sb("w_scales", [P, K], U8)
        nc.vector.quantize_mx(
            out=w_words[:].bitcast(FP8X4), scales=w_scales[:], in_=grouped_bf[:].rearrange("p k t -> p (k t)")
        )

        half_cols = I // 32
        listed_tags = ("scaled3", "least3", "prob3", "val_pool2")
        woven_early = sb("val_woven_early", [P, 3, P * PACK], BF16)
        woven_last = sb("val_woven_last", [P, 1, P * PACK], BF16)
        for j in range(4):
            listed = sb("val_listed%d" % j, [P, I], BF16, tag=listed_tags[j])
            window = val_pools[j][:]
            if j < 2:
                nc.scalar.activation(out=listed[:], in_=window.indirect(offsets[:]), func=ACT.Copy)
            elif j == 2:
                nc.vector.tensor_copy(out=listed[:], in_=window.indirect(offsets[:]))
            else:
                nc.scalar.activation(
                    out=listed[:, : I // 2], in_=window.indirect(offsets[:, :half_cols]), func=ACT.Copy
                )
                nc.vector.tensor_copy(out=listed[:, I // 2 :], in_=window.indirect(offsets[:, half_cols:]))
            pairs = listed[:].bitcast(F32)
            turned = bank("val_turned%d" % j, [P, 2, P], "score%d" % (1 + j % 3))
            for u in range(2):
                nc.tensor.transpose(turned[:, u, :], pairs[:, u::2], ident[:])
            woven = woven_early[:, j, :] if j < 3 else woven_last[:, 0, :]
            nc.scalar.copy(
                out=woven.bitcast(F32).rearrange("p (r u) -> p r u", u=2), in_=turned[:].rearrange("p u r -> p r u")
            )
        val_operands = []
        for name, woven, tiles, tag in (("early", woven_early, 3, "grouped"), ("last", woven_last, 1, None)):
            words = sb("val_words_" + name, [P, tiles * P], U32, tag=tag)
            scales = sb("val_scales_" + name, [P, tiles * P], U8)
            nc.vector.quantize_mx(
                out=words[:].bitcast(FP8X4), scales=scales[:], in_=woven[:].rearrange("p j w -> p (j w)")
            )
            for j in range(tiles):
                val_operands.append((words[:, j * P : (j + 1) * P], scales[:, j * P : (j + 1) * P]))

        result = bank("result", [P, 4, K], "dist0")
        for j, (words, scales) in enumerate(val_operands):
            nc.tensor.matmul_mx(
                out=result[:, j, :],
                lhsT=words.bitcast(FP8X4),
                lhsT_scale=scales,
                rhs=w_words[:].bitcast(FP8X4),
                rhs_scale=w_scales[:],
                start=True,
                stop=True,
            )
        result_sb = sb("result_sb", [P, 4, K], F32)
        nc.scalar.copy(out=result_sb[:], in_=result[:])
        nc.sync.dma_start(out=out.rearrange("(r j) k -> r j k", j=4), in_=result_sb[:])
